import numpy as np
import ml_dtypes


def mxq(x, axis, fmt="e4m3"):
    dtype, down = {"e4m3": (ml_dtypes.float8_e4m3fn, 7), "e5m2": (ml_dtypes.float8_e5m2, 14)}[fmt]
    v = np.moveaxis(np.asarray(x, np.float32).astype(ml_dtypes.bfloat16).astype(np.float64), axis, -1)
    blocks = v.reshape(v.shape[:-1] + (-1, 32))
    amax = np.abs(blocks).max(-1, keepdims=True)
    byte = np.maximum(np.where(amax > 0, np.frexp(amax)[1] - 1 + 127, 0) - down, 1)
    scale = np.exp2(byte - 127.0)
    codes = (blocks / scale).astype(np.float32).astype(dtype).astype(np.float64)
    return np.moveaxis((codes * scale).reshape(v.shape), -1, axis)


WIDE = False


def mx_kscale(k):
    if not WIDE:
        return np.ones(k)
    levels = np.array([30, -30])
    if k % 512:
        return np.exp2(np.random.permutation(np.resize(levels, k // 32))).repeat(32)
    a = np.empty((k // 512, 16))
    for p in range(k // 512):
        a[p, :8] = np.random.permutation(np.resize(levels, 8))
        for g in range(8):
            far = levels[np.abs(levels - a[p, g]) >= 10]
            a[p, g + 8] = far[np.random.randint(len(far))]
    return np.exp2(a.ravel()).repeat(32)


def f64(x):
    return np.asarray(x).astype(np.float64)


def striped(idx):
    return np.tile(np.asarray(idx).reshape(-1, 16).T, (8, 1)).astype(np.uint16)


def unstriped(offs):
    return offs[:16].T.reshape(-1).astype(np.int64)


E2M1 = np.array([0.0, 0.5, 1.0, 1.5, 2.0, 3.0, 4.0, 6.0, -0.0, -0.5, -1.0, -1.5, -2.0, -3.0, -4.0, -6.0])


def pack_weight(w, fmt):
    k, n = w.shape
    w = f64(np.asarray(w, np.float32).astype(ml_dtypes.bfloat16)).reshape(k // 32, 32, n)
    amax = np.abs(w).max(1)
    if fmt in ("e4m3", "e5m2"):
        byte = np.frexp(amax)[1] - 1 + 127 - (7 if fmt == "e4m3" else 14)
    else:
        mant, ex = np.frexp(amax / 6.0)
        byte = np.where(mant > 0.5, ex, ex - 1) + 127
    byte = np.clip(np.where(amax > 0, byte, 1), 1, 254)
    scaled = (w * np.exp2(127.0 - byte)[:, None, :]).reshape(k, n).astype(np.float32)
    by_word = np.ascontiguousarray(scaled.reshape(k // 512, 128, 4, n).transpose(0, 1, 3, 2))
    if fmt in ("e4m3", "e5m2"):
        words = by_word.astype(ml_dtypes.float8_e4m3fn if fmt == "e4m3" else ml_dtypes.float8_e5m2).view(np.uint8)
    else:
        c = by_word.astype(ml_dtypes.float4_e2m1fn).view(np.uint8) & 0xF
        words = (c[..., 0::2] | (c[..., 1::2] << 4)).reshape(k // 512, 128, 2 * n)
    return np.ascontiguousarray(words), np.ascontiguousarray(byte.astype(np.uint8).reshape(k // 512, 16, n))


def unpack_weight(words, scales, fmt):
    g, _, n = scales.shape
    words = np.ascontiguousarray(words).reshape(g, 128, n, -1)
    if fmt in ("e4m3", "e5m2"):
        vals = words.view(ml_dtypes.float8_e4m3fn if fmt == "e4m3" else ml_dtypes.float8_e5m2).astype(np.float64)
    else:
        nib = np.empty((g, 128, n, 4), np.uint8)
        nib[..., 0::2] = words & 0xF
        nib[..., 1::2] = words >> 4
        vals = E2M1[nib]
    vals = vals * np.repeat(np.exp2(scales.astype(np.float64) - 127.0), 8, axis=1)[..., None]
    return vals.transpose(0, 1, 3, 2).reshape(g * 512, n)


def sigmoid(v):
    return 1.0 / (1.0 + np.exp(-v))


def sgn(shape):
    return np.random.uniform(0.5, 2.0, shape) * np.where(np.random.standard_normal(shape) < 0, -1.0, 1.0)


K, T, J, R, F, Z, O, N, E = 512, 1024, 256, 512, 512, 1024, 128, 256, 512


def setup_inputs():
    n = np.random.standard_normal
    idx = np.random.permutation(T)[:J]
    idx2 = np.random.permutation(Z)[:J]
    idx3 = np.random.permutation(J)[:O]
    idx4 = np.random.permutation(J)[:O]
    idx5 = np.random.permutation(E)[:O]
    idx6 = np.random.permutation(E)[:O]
    fk = mx_kscale(K)
    ff = mx_kscale(F)
    fr = mx_kscale(R)
    xtp = pack_weight(n((K, T)) / fk[:, None], "e4m3")
    xop = pack_weight(n((F, Z)) / ff[:, None], "e2m1")
    wp = pack_weight(n((K, R)) * 1 / np.sqrt(K) * fk[:, None], "e2m1")
    w0p = pack_weight(n((F, R)) * 1 / np.sqrt(F) * ff[:, None], "e5m2")
    wbp = pack_weight(n((R, N)) * 1 / np.sqrt(R) / fr[:, None], "e5m2")
    return {
        "xt_words": xtp[0],
        "xt_scales": xtp[1],
        "xo_words": xop[0],
        "xo_scales": xop[1],
        "w_words": wp[0],
        "w_scales": wp[1],
        "w0_words": w0p[0],
        "w0_scales": w0p[1],
        "sa": (np.random.uniform(0.5, 1.6, (R, 1)) * fr[:, None]).astype(np.float32),
        "sg": (sgn((R, 1))).astype(np.float32),
        "bg": (np.random.uniform(-2.0, 2.0, (R, 1))).astype(np.float32),
        "wb_words": wbp[0],
        "wb_scales": wbp[1],
        "offs": striped(idx),
        "offs2": striped(idx2),
        "offs3": striped(idx3),
        "offs4": striped(idx4),
        "offs5": striped(idx5),
        "offs6": striped(idx6),
    }


def reference(xt_words, xt_scales, xo_words, xo_scales, w_words, w_scales, w0_words, w0_scales, sa, sg, bg, wb_words, wb_scales, offs, offs2, offs3, offs4, offs5, offs6):
    idx = unstriped(offs)
    idx2 = unstriped(offs2)
    idx3 = unstriped(offs3)
    idx4 = unstriped(offs4)
    idx5 = unstriped(offs5)
    idx6 = unstriped(offs6)
    xtu = unpack_weight(xt_words, xt_scales, "e4m3")
    xou = unpack_weight(xo_words, xo_scales, "e2m1")
    wu = unpack_weight(w_words, w_scales, "e2m1")
    w0u = unpack_weight(w0_words, w0_scales, "e5m2")
    wbu = unpack_weight(wb_words, wb_scales, "e5m2")
    xtidxg = xtu[:, idx]
    xoidx2g = xou[:, idx2]
    a = wu.T @ xtidxg + w0u.T @ xoidx2g
    hid = a[:, idx3] * f64(sa) * sigmoid(a[:, idx4] * f64(sg) + f64(bg))
    hidq = mxq(hid, 0, "e4m3")
    p = wbu.T @ hidq
    pa = np.zeros((N, E))
    pa[:, idx5] = p
    pb = np.zeros((N, E))
    pb[:, idx6] = p
    y = pa + pb
    return y

@@ -1,0 +1,141 @@
+from contextlib import ExitStack
+
+import concourse.mybir as mybir
+
+K, T, J, R, F, Z, O, N, E = 512, 1024, 256, 512, 512, 1024, 128, 256, 512
+FLOPS = 2 * K * R * J + 2 * F * R * J + 2 * R * N * O
+
+F32 = mybir.dt.float32
+BF16 = mybir.dt.bfloat16
+I32 = mybir.dt.int32
+U32 = mybir.dt.uint32
+U16 = mybir.dt.uint16
+U8 = mybir.dt.uint8
+E4M3 = mybir.dt.float8_e4m3fn_x4
+E5M2 = mybir.dt.float8_e5m2_x4
+E2M1 = mybir.dt.float4_e2m1fn_x4
+ACT = mybir.ActivationFunctionType
+ALU = mybir.AluOpType
+
+P = 128
+PACK = 4
+
+
+def load_scales(queue, plane, scales):
+    words = scales[0].bitcast(I32)
+    width = words.shape[1]
+    for q in range(4):
+        rows = words[4 * q:4 * q + 4, :].unsqueeze(0).to_broadcast([8, 4, width])
+        queue.dma_start(out=plane[32 * q:32 * q + 32, :].bitcast(I32), in_=rows)
+
+
+def tile_list_gatedpick_bank_one_pagetwice_kernel(tc, xt_words, xt_scales, xo_words, xo_scales, w_words, w_scales, w0_words, w0_scales, sa, sg, bg, wb_words, wb_scales, offs, offs2, offs3, offs4, offs5, offs6, out):
+    nc = tc.nc
+    with ExitStack() as ctx:
+        sb = ctx.enter_context(tc.tile_pool(name="sb", bufs=1))
+        ps = ctx.enter_context(tc.psum_pool(name="ps", bufs=1))
+
+        l1 = sb.tile([P, J // 16], U16, name="l1")
+        l2 = sb.tile([P, J // 16], U16, name="l2")
+        l3 = sb.tile([P, O // 16], U16, name="l3")
+        l4 = sb.tile([P, O // 16], U16, name="l4")
+        l5 = sb.tile([P, O // 16], U16, name="l5")
+        l6 = sb.tile([P, O // 16], U16, name="l6")
+        xt_w = sb.tile([P, T], U32, name="xt_w", align_bytes=64)
+        xt_s = sb.tile([P, T], U8, name="xt_s", align_bytes=64)
+        xo_w = sb.tile([P, Z], U16, name="xo_w", align_bytes=64)
+        xo_s = sb.tile([P, Z], U8, name="xo_s", align_bytes=64)
+        w_w = sb.tile([P, R], U16, name="w_w", align_bytes=64)
+        w0_w = sb.tile([P, R], U32, name="w0_w", align_bytes=64)
+        wb_w = sb.tile([P, N], U32, name="wb_w", align_bytes=64)
+        wb_s = sb.tile([P, N], U8, name="wb_s", align_bytes=64)
+        sa_t = sb.tile([P, PACK], F32, name="sa_t")
+        sg_t = sb.tile([P, PACK], F32, name="sg_t")
+        bg_t = sb.tile([P, PACK], F32, name="bg_t")
+
+        ws_stage = sb.tile([4, 4, 2 * R], U8, name="ws_stage")
+        ws = sb.tile([P, 2 * R], U8, name="ws", align_bytes=64)
+        ws_p = sb.tile([P, 2 * R], U8, name="ws_p", align_bytes=64)
+        nc.gpsimd.dma_start(out=ws_stage[:, :, 0:R].bitcast(I32), in_=w_scales[0].bitcast(I32).rearrange("(q r) m -> r q m", r=4))
+        nc.gpsimd.dma_start(out=ws_stage[:, :, R:2 * R].bitcast(I32), in_=w0_scales[0].bitcast(I32).rearrange("(q r) m -> r q m", r=4))
+        nc.sync.dma_start(l1[:], offs)
+        load_scales(nc.scalar, xt_s, xt_scales)
+        nc.sync.dma_start(out=xt_w[:].bitcast(I32), in_=xt_words[0].rearrange("p n t -> p (n t)").bitcast(I32))
+        nc.sync.dma_start(l2[:], offs2)
+        nc.sync.dma_start(out=xo_w[:].bitcast(I32), in_=xo_words[0].bitcast(I32))
+        load_scales(nc.scalar, xo_s, xo_scales)
+        nc.sync.dma_start(out=w_w[:].bitcast(I32), in_=w_words[0].bitcast(I32))
+        nc.sync.dma_start(out=w0_w[:].bitcast(I32), in_=w0_words[0].rearrange("p n t -> p (n t)").bitcast(I32))
+        nc.sync.dma_start(l4[:], offs4)
+        nc.sync.dma_start(out=sg_t[:], in_=sg.rearrange("(p t) o -> p (t o)", t=PACK))
+        nc.sync.dma_start(out=bg_t[:], in_=bg.rearrange("(p t) o -> p (t o)", t=PACK))
+        nc.sync.dma_start(l3[:], offs3)
+        nc.sync.dma_start(out=sa_t[:], in_=sa.rearrange("(p t) o -> p (t o)", t=PACK))
+        nc.sync.dma_start(out=wb_w[:].bitcast(I32), in_=wb_words[0].rearrange("p n t -> p (n t)").bitcast(I32))
+        load_scales(nc.sync, wb_s, wb_scales)
+        nc.sync.dma_start(l5[:], offs5)
+        nc.sync.dma_start(l6[:], offs6)
+        nc.vector.memset(ws[:].bitcast(I32), 0)
+
+        pa = [sb.tile([P, E], F32, name="pa%d" % h) for h in range(2)]
+        pb = [sb.tile([P, E], F32, name="pb%d" % h) for h in range(2)]
+        for page in pa + pb:
+            nc.vector.memset(page[:], 0.0)
+
+        xt_gw = sb.tile([P, J], U32, name="xt_gw", align_bytes=64)
+        xt_gs = sb.tile([P, J], U8, name="xt_gs", align_bytes=64)
+        xo_gw = sb.tile([P, J], U16, name="xo_gw", align_bytes=64)
+        xo_gs = sb.tile([P, J], U8, name="xo_gs", align_bytes=64)
+        w_pw = sb.tile([P, R], U16, name="w_pw", align_bytes=64)
+        w0_pw = sb.tile([P, R], U32, name="w0_pw", align_bytes=64)
+
+        nc.scalar.copy(w_pw[:].rearrange("p (t m) -> p m t", t=PACK), w_w[:].rearrange("p (m t) -> p m t", t=PACK))
+        nc.scalar.copy(w0_pw[:].rearrange("p (t m) -> p m t", t=PACK), w0_w[:].rearrange("p (m t) -> p m t", t=PACK))
+        nc.vector.tensor_copy(xt_gs[:], xt_s[:].indirect(l1[:]))
+        nc.vector.tensor_copy(xt_gw[:], xt_w[:].indirect(l1[:]))
+        for q in range(4):
+            nc.vector.tensor_copy(ws[32 * q:32 * q + 4, :].bitcast(I32), ws_stage[:, q, :].bitcast(I32))
+        nc.vector.tensor_copy(ws_p[:].rearrange("p (i t m) -> p i t m", i=2, t=PACK), ws[:].rearrange("p (i m t) -> p i t m", i=2, t=PACK))
+        nc.vector.tensor_copy(xo_gs[:], xo_s[:].indirect(l2[:]))
+        nc.vector.tensor_copy(xo_gw[:], xo_w[:].indirect(l2[:]))
+
+        acc = [ps.tile([P, J], F32, name="acc%d" % t) for t in range(PACK)]
+        for t in range(PACK):
+            cols = slice(t * P, (t + 1) * P)
+            nc.tensor.matmul_mx(out=acc[t][:], lhsT=w_pw[:, cols].bitcast(E2M1), lhsT_scale=ws_p[:, cols],
+                                rhs=xt_gw[:].bitcast(E4M3), rhs_scale=xt_gs[:], start=True, stop=False)
+        for t in range(PACK):
+            cols = slice(t * P, (t + 1) * P)
+            nc.tensor.matmul_mx(out=acc[t][:], lhsT=w0_pw[:, cols].bitcast(E5M2), lhsT_scale=ws_p[:, R + t * P:R + (t + 1) * P],
+                                rhs=xo_gw[:].bitcast(E2M1), rhs_scale=xo_gs[:], start=False, stop=True)
+
+        a = [sb.tile([P, J], F32, name="a%d" % t) for t in range(PACK)]
+        gate = [sb.tile([P, O], F32, name="gate%d" % t) for t in range(PACK)]
+        val = [sb.tile([P, O], F32, name="val%d" % t) for t in range(PACK)]
+        hid = sb.tile([P, O, PACK], BF16, name="hid", align_bytes=64)
+        for t in range(PACK):
+            nc.vector.tensor_copy(a[t][:], acc[t][:])
+        for t in range(PACK):
+            nc.scalar.activation(out=gate[t][:], in_=a[t][:].indirect(l4[:]), func=ACT.Sigmoid,
+                                 bias=bg_t[:, t:t + 1], scale=sg_t[:, t:t + 1])
+            nc.scalar.activation(out=val[t][:], in_=a[t][:].indirect(l3[:]), func=ACT.Copy, scale=sa_t[:, t:t + 1])
+            nc.vector.tensor_tensor(hid[:, :, t], val[t][:], gate[t][:], ALU.mult)
+
+        hq_w = sb.tile([P, O], U32, name="hq_w", align_bytes=64)
+        hq_s = sb.tile([P, O], U8, name="hq_s", align_bytes=64)
+        nc.vector.quantize_mx(out=hq_w[:].bitcast(E4M3), scales=hq_s[:], in_=hid[:].rearrange("p o t -> p (o t)"))
+
+        prod = [ps.tile([P, O], F32, name="prod%d" % h) for h in range(2)]
+        p_sb = [sb.tile([P, O], F32, name="p_sb%d" % h) for h in range(2)]
+        y = [sb.tile([P, E], F32, name="y%d" % h) for h in range(2)]
+        for h in range(2):
+            cols = slice(h * P, (h + 1) * P)
+            nc.tensor.matmul_mx(out=prod[h][:], lhsT=wb_w[:, cols].bitcast(E5M2), lhsT_scale=wb_s[:, cols],
+                                rhs=hq_w[:].bitcast(E4M3), rhs_scale=hq_s[:], start=True, stop=True)
+        nc.vector.tensor_copy(p_sb[0][:], prod[0][:])
+        nc.scalar.copy(p_sb[1][:], prod[1][:])
+        for h in range(2):
+            nc.vector.tensor_copy(pa[h][:].indirect(l5[:]), p_sb[h][:])
+            nc.scalar.activation(out=pb[h][:].indirect(l6[:]), in_=p_sb[h][:], func=ACT.Copy)
+            nc.vector.tensor_tensor(y[h][:], pa[h][:], pb[h][:], ALU.add)
+            nc.sync.dma_start(out=out[h * P:(h + 1) * P, :], in_=y[h][:])

@@ -21,10 +21,10 @@ P = 128
 PACK = 4
 
 
-def load_scales(queue, plane, scales):
+def load_scales(queue, plane, scales, quads=range(4)):
     words = scales[0].bitcast(I32)
     width = words.shape[1]
-    for q in range(4):
+    for q in quads:
         rows = words[4 * q:4 * q + 4, :].unsqueeze(0).to_broadcast([8, 4, width])
         queue.dma_start(out=plane[32 * q:32 * q + 32, :].bitcast(I32), in_=rows)
 
@@ -55,17 +55,18 @@ def tile_list_gatedpick_bank_one_pagetwice_kernel(tc, xt_words, xt_scales, xo_wo
 
         ws_stage = sb.tile([4, 4, 2 * R], U8, name="ws_stage")
         ws = sb.tile([P, 2 * R], U8, name="ws", align_bytes=64)
-        ws_p = sb.tile([P, 2 * R], U8, name="ws_p", align_bytes=64)
-        nc.gpsimd.dma_start(out=ws_stage[:, :, 0:R].bitcast(I32), in_=w_scales[0].bitcast(I32).rearrange("(q r) m -> r q m", r=4))
-        nc.gpsimd.dma_start(out=ws_stage[:, :, R:2 * R].bitcast(I32), in_=w0_scales[0].bitcast(I32).rearrange("(q r) m -> r q m", r=4))
-        nc.sync.dma_start(l1[:], offs)
-        load_scales(nc.scalar, xt_s, xt_scales)
-        nc.sync.dma_start(out=xt_w[:].bitcast(I32), in_=xt_words[0].rearrange("p n t -> p (n t)").bitcast(I32))
+        ws_p = [sb.tile([P, 2, P], U8, name="ws_p%d" % t, align_bytes=64) for t in range(PACK)]
         nc.sync.dma_start(l2[:], offs2)
+        nc.scalar.dma_start(out=ws_stage[:, :, R:2 * R].bitcast(I32), in_=w0_scales[0].bitcast(I32).rearrange("(q r) m -> r q m", r=4))
+        nc.sync.dma_start(l1[:], offs)
+        nc.scalar.dma_start(out=ws_stage[:, :, 0:R].bitcast(I32), in_=w_scales[0].bitcast(I32).rearrange("(q r) m -> r q m", r=4))
         nc.sync.dma_start(out=xo_w[:].bitcast(I32), in_=xo_words[0].bitcast(I32))
-        load_scales(nc.scalar, xo_s, xo_scales)
-        nc.sync.dma_start(out=w_w[:].bitcast(I32), in_=w_words[0].bitcast(I32))
+        load_scales(nc.scalar, xo_s, xo_scales, (0, 1))
+        nc.sync.dma_start(out=xt_w[:].bitcast(I32), in_=xt_words[0].rearrange("p n t -> p (n t)").bitcast(I32))
         nc.sync.dma_start(out=w0_w[:].bitcast(I32), in_=w0_words[0].rearrange("p n t -> p (n t)").bitcast(I32))
+        nc.sync.dma_start(out=w_w[:].bitcast(I32), in_=w_words[0].bitcast(I32))
+        load_scales(nc.sync, xo_s, xo_scales, (2, 3))
+        load_scales(nc.sync, xt_s, xt_scales)
         nc.sync.dma_start(l4[:], offs4)
         nc.sync.dma_start(out=sg_t[:], in_=sg.rearrange("(p t) o -> p (t o)", t=PACK))
         nc.sync.dma_start(out=bg_t[:], in_=bg.rearrange("(p t) o -> p (t o)", t=PACK))
@@ -89,37 +90,38 @@ def tile_list_gatedpick_bank_one_pagetwice_kernel(tc, xt_words, xt_scales, xo_wo
         w_pw = sb.tile([P, R], U16, name="w_pw", align_bytes=64)
         w0_pw = sb.tile([P, R], U32, name="w0_pw", align_bytes=64)
 
-        nc.scalar.copy(w_pw[:].rearrange("p (t m) -> p m t", t=PACK), w_w[:].rearrange("p (m t) -> p m t", t=PACK))
         nc.scalar.copy(w0_pw[:].rearrange("p (t m) -> p m t", t=PACK), w0_w[:].rearrange("p (m t) -> p m t", t=PACK))
-        nc.vector.tensor_copy(xt_gs[:], xt_s[:].indirect(l1[:]))
-        nc.vector.tensor_copy(xt_gw[:], xt_w[:].indirect(l1[:]))
+        nc.scalar.copy(w_pw[:].rearrange("p (t m) -> p m t", t=PACK), w_w[:].rearrange("p (m t) -> p m t", t=PACK))
         for q in range(4):
             nc.vector.tensor_copy(ws[32 * q:32 * q + 4, :].bitcast(I32), ws_stage[:, q, :].bitcast(I32))
-        nc.vector.tensor_copy(ws_p[:].rearrange("p (i t m) -> p i t m", i=2, t=PACK), ws[:].rearrange("p (i m t) -> p i t m", i=2, t=PACK))
-        nc.vector.tensor_copy(xo_gs[:], xo_s[:].indirect(l2[:]))
+        for t in range(PACK):
+            nc.gpsimd.tensor_copy(ws_p[t][:], ws[:].rearrange("p (i m t) -> p t i m", i=2, t=PACK)[:, t])
         nc.vector.tensor_copy(xo_gw[:], xo_w[:].indirect(l2[:]))
+        nc.vector.tensor_copy(xt_gw[:], xt_w[:].indirect(l1[:]))
+        nc.vector.tensor_copy(xo_gs[:], xo_s[:].indirect(l2[:]))
+        nc.vector.tensor_copy(xt_gs[:], xt_s[:].indirect(l1[:]))
 
         acc = [ps.tile([P, J], F32, name="acc%d" % t) for t in range(PACK)]
         for t in range(PACK):
             cols = slice(t * P, (t + 1) * P)
-            nc.tensor.matmul_mx(out=acc[t][:], lhsT=w_pw[:, cols].bitcast(E2M1), lhsT_scale=ws_p[:, cols],
-                                rhs=xt_gw[:].bitcast(E4M3), rhs_scale=xt_gs[:], start=True, stop=False)
-        for t in range(PACK):
-            cols = slice(t * P, (t + 1) * P)
-            nc.tensor.matmul_mx(out=acc[t][:], lhsT=w0_pw[:, cols].bitcast(E5M2), lhsT_scale=ws_p[:, R + t * P:R + (t + 1) * P],
-                                rhs=xo_gw[:].bitcast(E2M1), rhs_scale=xo_gs[:], start=False, stop=True)
+            nc.tensor.matmul_mx(out=acc[t][:], lhsT=w0_pw[:, cols].bitcast(E5M2), lhsT_scale=ws_p[t][:, 1, :],
+                                rhs=xo_gw[:].bitcast(E2M1), rhs_scale=xo_gs[:], start=True, stop=False)
+            nc.tensor.matmul_mx(out=acc[t][:], lhsT=w_pw[:, cols].bitcast(E2M1), lhsT_scale=ws_p[t][:, 0, :],
+                                rhs=xt_gw[:].bitcast(E4M3), rhs_scale=xt_gs[:], start=False, stop=True)
 
         a = [sb.tile([P, J], F32, name="a%d" % t) for t in range(PACK)]
-        gate = [sb.tile([P, O], F32, name="gate%d" % t) for t in range(PACK)]
-        val = [sb.tile([P, O], F32, name="val%d" % t) for t in range(PACK)]
+        gate = [sb.tile([P, 2, O], F32, name="gate%d" % u) for u in range(2)]
+        val = [sb.tile([P, 2, O], F32, name="val%d" % u) for u in range(2)]
         hid = sb.tile([P, O, PACK], BF16, name="hid", align_bytes=64)
         for t in range(PACK):
             nc.vector.tensor_copy(a[t][:], acc[t][:])
         for t in range(PACK):
-            nc.scalar.activation(out=gate[t][:], in_=a[t][:].indirect(l4[:]), func=ACT.Sigmoid,
+            nc.scalar.activation(out=gate[t // 2][:, t % 2, :], in_=a[t][:].indirect(l4[:]), func=ACT.Sigmoid,
                                  bias=bg_t[:, t:t + 1], scale=sg_t[:, t:t + 1])
-            nc.scalar.activation(out=val[t][:], in_=a[t][:].indirect(l3[:]), func=ACT.Copy, scale=sa_t[:, t:t + 1])
-            nc.vector.tensor_tensor(hid[:, :, t], val[t][:], gate[t][:], ALU.mult)
+            nc.scalar.activation(out=val[t // 2][:, t % 2, :], in_=a[t][:].indirect(l3[:]), func=ACT.Copy, scale=sa_t[:, t:t + 1])
+            if t % 2 == 1:
+                nc.vector.tensor_tensor(hid[:, :, t - 1:t + 1], val[t // 2][:].rearrange("p e o -> p o e"),
+                                        gate[t // 2][:].rearrange("p e o -> p o e"), ALU.mult)
 
         hq_w = sb.tile([P, O], U32, name="hq_w", align_bytes=64)
         hq_s = sb.tile([P, O], U8, name="hq_s", align_bytes=64)
@@ -137,5 +139,6 @@ def tile_list_gatedpick_bank_one_pagetwice_kernel(tc, xt_words, xt_scales, xo_wo
         for h in range(2):
             nc.vector.tensor_copy(pa[h][:].indirect(l5[:]), p_sb[h][:])
             nc.scalar.activation(out=pb[h][:].indirect(l6[:]), in_=p_sb[h][:], func=ACT.Copy)
-            nc.vector.tensor_tensor(y[h][:], pa[h][:], pb[h][:], ALU.add)
-            nc.sync.dma_start(out=out[h * P:(h + 1) * P, :], in_=y[h][:])
+            for cols in (slice(0, E),) if h == 0 else (slice(0, 384), slice(384, E)):
+                nc.vector.tensor_tensor(y[h][:, cols], pa[h][:, cols], pb[h][:, cols], ALU.add)
+                nc.sync.dma_start(out=out[h * P:(h + 1) * P, cols], in_=y[h][:, cols])

from contextlib import ExitStack

import concourse.mybir as mybir

K, T, J, R, F, Z, O, N, E = 512, 1024, 256, 512, 512, 1024, 128, 256, 512
FLOPS = 2 * K * R * J + 2 * F * R * J + 2 * R * N * O

F32 = mybir.dt.float32
BF16 = mybir.dt.bfloat16
I32 = mybir.dt.int32
U32 = mybir.dt.uint32
U16 = mybir.dt.uint16
U8 = mybir.dt.uint8
E4M3 = mybir.dt.float8_e4m3fn_x4
E5M2 = mybir.dt.float8_e5m2_x4
E2M1 = mybir.dt.float4_e2m1fn_x4
ACT = mybir.ActivationFunctionType
ALU = mybir.AluOpType

P = 128
PACK = 4


def load_scales(queue, plane, scales, quads=range(4)):
    words = scales[0].bitcast(I32)
    width = words.shape[1]
    for q in quads:
        rows = words[4 * q:4 * q + 4, :].unsqueeze(0).to_broadcast([8, 4, width])
        queue.dma_start(out=plane[32 * q:32 * q + 32, :].bitcast(I32), in_=rows)


def tile_list_gatedpick_bank_one_pagetwice_kernel(tc, xt_words, xt_scales, xo_words, xo_scales, w_words, w_scales, w0_words, w0_scales, sa, sg, bg, wb_words, wb_scales, offs, offs2, offs3, offs4, offs5, offs6, out):
    nc = tc.nc
    with ExitStack() as ctx:
        sb = ctx.enter_context(tc.tile_pool(name="sb", bufs=1))
        ps = ctx.enter_context(tc.psum_pool(name="ps", bufs=1))

        l1 = sb.tile([P, J // 16], U16, name="l1")
        l2 = sb.tile([P, J // 16], U16, name="l2")
        l3 = sb.tile([P, O // 16], U16, name="l3")
        l4 = sb.tile([P, O // 16], U16, name="l4")
        l5 = sb.tile([P, O // 16], U16, name="l5")
        l6 = sb.tile([P, O // 16], U16, name="l6")
        xt_w = sb.tile([P, T], U32, name="xt_w", align_bytes=64)
        xt_s = sb.tile([P, T], U8, name="xt_s", align_bytes=64)
        xo_w = sb.tile([P, Z], U16, name="xo_w", align_bytes=64)
        xo_s = sb.tile([P, Z], U8, name="xo_s", align_bytes=64)
        w_w = sb.tile([P, R], U16, name="w_w", align_bytes=64)
        w0_w = sb.tile([P, R], U32, name="w0_w", align_bytes=64)
        wb_w = sb.tile([P, N], U32, name="wb_w", align_bytes=64)
        wb_s = sb.tile([P, N], U8, name="wb_s", align_bytes=64)
        sa_t = sb.tile([P, PACK], F32, name="sa_t")
        sg_t = sb.tile([P, PACK], F32, name="sg_t")
        bg_t = sb.tile([P, PACK], F32, name="bg_t")

        ws_stage = sb.tile([4, 4, 2 * R], U8, name="ws_stage")
        ws = sb.tile([P, 2 * R], U8, name="ws", align_bytes=64)
        ws_p = [sb.tile([P, 2, P], U8, name="ws_p%d" % t, align_bytes=64) for t in range(PACK)]
        nc.sync.dma_start(l2[:], offs2)
        nc.scalar.dma_start(out=ws_stage[:, :, R:2 * R].bitcast(I32), in_=w0_scales[0].bitcast(I32).rearrange("(q r) m -> r q m", r=4))
        nc.sync.dma_start(l1[:], offs)
        nc.scalar.dma_start(out=ws_stage[:, :, 0:R].bitcast(I32), in_=w_scales[0].bitcast(I32).rearrange("(q r) m -> r q m", r=4))
        nc.sync.dma_start(out=xo_w[:].bitcast(I32), in_=xo_words[0].bitcast(I32))
        load_scales(nc.scalar, xo_s, xo_scales, (0, 1))
        nc.sync.dma_start(out=xt_w[:].bitcast(I32), in_=xt_words[0].rearrange("p n t -> p (n t)").bitcast(I32))
        nc.sync.dma_start(out=w0_w[:].bitcast(I32), in_=w0_words[0].rearrange("p n t -> p (n t)").bitcast(I32))
        nc.sync.dma_start(out=w_w[:].bitcast(I32), in_=w_words[0].bitcast(I32))
        load_scales(nc.sync, xo_s, xo_scales, (2, 3))
        load_scales(nc.sync, xt_s, xt_scales)
        nc.sync.dma_start(l4[:], offs4)
        nc.sync.dma_start(out=sg_t[:], in_=sg.rearrange("(p t) o -> p (t o)", t=PACK))
        nc.sync.dma_start(out=bg_t[:], in_=bg.rearrange("(p t) o -> p (t o)", t=PACK))
        nc.sync.dma_start(l3[:], offs3)
        nc.sync.dma_start(out=sa_t[:], in_=sa.rearrange("(p t) o -> p (t o)", t=PACK))
        nc.sync.dma_start(out=wb_w[:].bitcast(I32), in_=wb_words[0].rearrange("p n t -> p (n t)").bitcast(I32))
        load_scales(nc.sync, wb_s, wb_scales)
        nc.sync.dma_start(l5[:], offs5)
        nc.sync.dma_start(l6[:], offs6)
        nc.vector.memset(ws[:].bitcast(I32), 0)

        pa = [sb.tile([P, E], F32, name="pa%d" % h) for h in range(2)]
        pb = [sb.tile([P, E], F32, name="pb%d" % h) for h in range(2)]
        for page in pa + pb:
            nc.vector.memset(page[:], 0.0)

        xt_gw = sb.tile([P, J], U32, name="xt_gw", align_bytes=64)
        xt_gs = sb.tile([P, J], U8, name="xt_gs", align_bytes=64)
        xo_gw = sb.tile([P, J], U16, name="xo_gw", align_bytes=64)
        xo_gs = sb.tile([P, J], U8, name="xo_gs", align_bytes=64)
        w_pw = sb.tile([P, R], U16, name="w_pw", align_bytes=64)
        w0_pw = sb.tile([P, R], U32, name="w0_pw", align_bytes=64)

        nc.scalar.copy(w0_pw[:].rearrange("p (t m) -> p m t", t=PACK), w0_w[:].rearrange("p (m t) -> p m t", t=PACK))
        nc.scalar.copy(w_pw[:].rearrange("p (t m) -> p m t", t=PACK), w_w[:].rearrange("p (m t) -> p m t", t=PACK))
        for q in range(4):
            nc.vector.tensor_copy(ws[32 * q:32 * q + 4, :].bitcast(I32), ws_stage[:, q, :].bitcast(I32))
        for t in range(PACK):
            nc.gpsimd.tensor_copy(ws_p[t][:], ws[:].rearrange("p (i m t) -> p t i m", i=2, t=PACK)[:, t])
        nc.vector.tensor_copy(xo_gw[:], xo_w[:].indirect(l2[:]))
        nc.vector.tensor_copy(xt_gw[:], xt_w[:].indirect(l1[:]))
        nc.vector.tensor_copy(xo_gs[:], xo_s[:].indirect(l2[:]))
        nc.vector.tensor_copy(xt_gs[:], xt_s[:].indirect(l1[:]))

        acc = [ps.tile([P, J], F32, name="acc%d" % t) for t in range(PACK)]
        for t in range(PACK):
            cols = slice(t * P, (t + 1) * P)
            nc.tensor.matmul_mx(out=acc[t][:], lhsT=w0_pw[:, cols].bitcast(E5M2), lhsT_scale=ws_p[t][:, 1, :],
                                rhs=xo_gw[:].bitcast(E2M1), rhs_scale=xo_gs[:], start=True, stop=False)
            nc.tensor.matmul_mx(out=acc[t][:], lhsT=w_pw[:, cols].bitcast(E2M1), lhsT_scale=ws_p[t][:, 0, :],
                                rhs=xt_gw[:].bitcast(E4M3), rhs_scale=xt_gs[:], start=False, stop=True)

        a = [sb.tile([P, J], F32, name="a%d" % t) for t in range(PACK)]
        gate = [sb.tile([P, 2, O], F32, name="gate%d" % u) for u in range(2)]
        val = [sb.tile([P, 2, O], F32, name="val%d" % u) for u in range(2)]
        hid = sb.tile([P, O, PACK], BF16, name="hid", align_bytes=64)
        for t in range(PACK):
            nc.vector.tensor_copy(a[t][:], acc[t][:])
        for t in range(PACK):
            nc.scalar.activation(out=gate[t // 2][:, t % 2, :], in_=a[t][:].indirect(l4[:]), func=ACT.Sigmoid,
                                 bias=bg_t[:, t:t + 1], scale=sg_t[:, t:t + 1])
            nc.scalar.activation(out=val[t // 2][:, t % 2, :], in_=a[t][:].indirect(l3[:]), func=ACT.Copy, scale=sa_t[:, t:t + 1])
            if t % 2 == 1:
                nc.vector.tensor_tensor(hid[:, :, t - 1:t + 1], val[t // 2][:].rearrange("p e o -> p o e"),
                                        gate[t // 2][:].rearrange("p e o -> p o e"), ALU.mult)

        hq_w = sb.tile([P, O], U32, name="hq_w", align_bytes=64)
        hq_s = sb.tile([P, O], U8, name="hq_s", align_bytes=64)
        nc.vector.quantize_mx(out=hq_w[:].bitcast(E4M3), scales=hq_s[:], in_=hid[:].rearrange("p o t -> p (o t)"))

        prod = [ps.tile([P, O], F32, name="prod%d" % h) for h in range(2)]
        p_sb = [sb.tile([P, O], F32, name="p_sb%d" % h) for h in range(2)]
        y = [sb.tile([P, E], F32, name="y%d" % h) for h in range(2)]
        for h in range(2):
            cols = slice(h * P, (h + 1) * P)
            nc.tensor.matmul_mx(out=prod[h][:], lhsT=wb_w[:, cols].bitcast(E5M2), lhsT_scale=wb_s[:, cols],
                                rhs=hq_w[:].bitcast(E4M3), rhs_scale=hq_s[:], start=True, stop=True)
        nc.vector.tensor_copy(p_sb[0][:], prod[0][:])
        nc.scalar.copy(p_sb[1][:], prod[1][:])
        for h in range(2):
            nc.vector.tensor_copy(pa[h][:].indirect(l5[:]), p_sb[h][:])
            nc.scalar.activation(out=pb[h][:].indirect(l6[:]), in_=p_sb[h][:], func=ACT.Copy)
            for cols in (slice(0, E),) if h == 0 else (slice(0, 384), slice(384, E)):
                nc.vector.tensor_tensor(y[h][:, cols], pa[h][:, cols], pb[h][:, cols], ALU.add)
                nc.sync.dma_start(out=out[h * P:(h + 1) * P, cols], in_=y[h][:, cols])
